import numpy as np
CORES = [100,101,102,103,108,109,110,111]
N = 8
T, CAP = 256, 32
def entries(a): return a.T.reshape(-1)
def pack(v, P): return np.ascontiguousarray(np.asarray(v, np.int32).reshape(-1, P).T)
def lists(rng, how):
    L = rng.integers(0, T, (N, N, CAP))
    if how == "alike": L[:] = rng.integers(0, T, (N, N, 1))
    if how == "distinct": L = np.stack([np.stack([rng.permutation(T)[:CAP] for d in range(N)]) for r in range(N)])
    if how == "sorted": L = np.sort(L, axis=2)
    if how == "edge": L = np.where(rng.random((N, N, CAP)) < 0.5, 0, T - 1)
    return {"l": np.stack([pack(L[r].reshape(-1), 16) for r in range(N)])}
def setup_inputs(rng):
    return dict({"x": rng.standard_normal((N, 128, T), dtype=np.float32)}, **lists(rng, "uniform"))
def setup_inputs_alike(rng):
    d = setup_inputs(rng); d.update(lists(rng, "alike"))
    for k in ("x",): d[k] = (d[k].astype(np.float32) * 1048576.0).astype(d[k].dtype)
    return d
def setup_inputs_distinct(rng):
    d = setup_inputs(rng); d.update(lists(rng, "distinct"))
    for k in ("x",): d[k] = (d[k].astype(np.float32) * (1 / 1024.0)).astype(d[k].dtype)
    return d
def setup_inputs_edge(rng):
    d = setup_inputs(rng); d.update(lists(rng, "edge"))
    return d
def setup_inputs_sorted(rng):
    d = setup_inputs(rng); d.update(lists(rng, "sorted"))
    return d
def check_inputs(x):
    bad = []
    if x["l"].min() < 0 or x["l"].max() >= T: bad.append("l out of range")
    return bad
def reference(x, l):
    y = np.zeros((N, 128, N * CAP), x.dtype)
    for r in range(N):
        L = entries(l[r])
        for d in range(N): y[d][:, CAP * r:CAP * r + CAP] = x[r][:, L[CAP * d:CAP * d + CAP]]
    return {"y": y}

@@ -1,0 +1,157 @@
+from concourse.bass import DstId, RemoteDMATransfer
+from concourse.mybir import AluOpType
+
+W = 32
+GRP = 16
+
+SCRATCH = {
+    "xs":    ("sbuf", [128, 256], "float32"),
+    "l32":   ("sbuf", [128, 16], "int32"),
+    "lf":    ("sbuf", [128, 16], "float32"),
+    "ones":  ("sbuf", [128, 128], "float32"),
+    "rep":   ("sbuf", [128, 128], "float32"),
+    "offp":  ("psum", [128, 16], "float32"),
+    "off":   ("sbuf", [128, 16], "uint16"),
+    "gath":  ("sbuf", [128, 256], "float32"),
+    "stage": ("sbuf", [128, 128], "float32"),
+    "land":  ("sbuf", [128, 256], "float32"),
+}
+SEMAPHORES = ["s_x", "s_l", "s_one", "s_rep", "s_lf", "s_mm", "s_off", "s_gf", "s_gn", "s_own",
+              "near", "fard", "farr", "rel", "sent", "st_a", "st_b", "st_c"]
+
+
+def _bits(mask):
+    return [e for e in range(mask.bit_length()) if (mask >> e) & 1]
+
+
+def _mask(engines):
+    m = 0
+    for e in engines:
+        m |= 1 << e
+    return m
+
+
+def _runs(ranks):
+    out = []
+    for r in sorted(ranks):
+        if out and out[-1][1] == r:
+            out[-1][1] = r + 1
+        else:
+            out.append([r, r + 1])
+    return [(a, b) for a, b in out]
+
+
+def rank_program(g, core, T, topo):
+    rank = T.rank_of(core)
+    if rank is None:
+        return
+    cores = list(T.cores)
+    n = len(cores)
+    sem = T.sem
+
+    def chipmates(r):
+        return [q for q in range(n) if topo.chip(cores[q]) == topo.chip(cores[r])]
+
+    def others(r):
+        return [q for q in range(n) if topo.chip(cores[q]) != topo.chip(cores[r])]
+
+    def direct(r):
+        return all(topo.may_write(cores[r], cores[q]) for q in others(r))
+
+    def gate(r):
+        if direct(r):
+            return r
+        ports = [q for q in chipmates(r) if direct(q)]
+        rest = [q for q in chipmates(r) if not direct(q)]
+        return ports[rest.index(r) % len(ports)]
+
+    home = chipmates(rank)
+    far = others(rank)
+    (f0, f1), = _runs(far)
+    (h0, h1), = _runs(home)
+    clients = [q for q in home if q != rank and gate(q) == rank]
+    assert len(clients) <= 1
+
+    def dst(r):
+        rid, pid, _ = topo.addr(cores[r])
+        return DstId(rid=rid, pnc=pid)
+
+    peers = [q for q in home if q != rank]
+    all_e = _bits(topo.mask(core, cores[peers[0]]))
+    out_e = _bits(topo.mask(core, cores[far[0]]))
+    in_e = [e for e in all_e if e not in out_e]
+    k_far = len(out_e) // len(far)
+    k_near = 2
+    k_stage = len(out_e)
+
+    g.sync.dma_start(T.xs[:, :], T.x[:, :]).then_inc(sem.s_x, 16)
+    g.scalar.dma_start(T.l32[0:GRP, :], T.l[:, :]).then_inc(sem.s_l, 16)
+
+    g.vector.memset(T.ones[0:GRP, :], 1.0).then_inc(sem.s_one, 1)
+    g.wait_ge(sem.s_one, 1)
+    g.affine_select(T.rep[0:GRP, :], T.ones[0:GRP, :], [[0, 128 // GRP], [-1, GRP]], AluOpType.is_equal, 0.0, 0,
+                    1).then_inc(sem.s_rep, 1)
+    g.vector.wait_ge(sem.s_l, 16)
+    g.vector.tensor_copy(T.lf[0:GRP, :], T.l32[0:GRP, :]).then_inc(sem.s_lf, 1)
+    g.tensor.wait_ge(sem.s_rep, 1)
+    g.tensor.wait_ge(sem.s_lf, 1)
+    g.tensor.matmul(T.offp[:, :], T.rep[0:GRP, :], T.lf[0:GRP, :], True, True).then_inc(sem.s_mm, 1)
+    g.vector.wait_ge(sem.s_mm, 1)
+    g.vector.tensor_copy(T.off[:, :], T.offp[:, :]).then_inc(sem.s_off, 1)
+
+    c = W // GRP
+    g.vector.wait_ge(sem.s_off, 1)
+    g.vector.wait_ge(sem.s_x, 16)
+    g.vector.tensor_copy(T.gath[:, W * f0:W * f1], T.xs[:, :].indirect(T.off[:, c * f0:c * f1])).then_inc(sem.s_gf, 1)
+    g.vector.tensor_copy(T.gath[:, W * h0:W * h1], T.xs[:, :].indirect(T.off[:, c * h0:c * h1])).then_inc(sem.s_gn, 1)
+    g.vector.tensor_copy(T.land[:, W * rank:W * rank + W],
+                         T.xs[:, :].indirect(T.off[:, c * rank:c * rank + c])).then_inc(sem.s_own, 1)
+
+    sent = 0
+    g.wait_ge(sem.s_gf, 1)
+    if direct(rank):
+        g.remote_dma_fused(
+            [RemoteDMATransfer(dst_ids=[dst(d)], dma_engine_mask=_mask(out_e[k_far * i:k_far * (i + 1)]),
+                               remote_sem=sem.fard, src=T.gath[:, W * d:W * d + W],
+                               dst=T.land[:, W * rank:W * rank + W]) for i, d in enumerate(far)],
+            local_sem=sem.sent)
+        sent += k_far * len(far)
+    else:
+        rid, pid, _ = topo.addr(cores[gate(rank)])
+        g.remote_dma(T.stage[:, :], T.gath[:, W * f0:W * f1], sem.rel, sem.sent, pid, rid, _mask(all_e[:k_stage]))
+        sent += k_stage
+    g.wait_ge(sem.s_gn, 1)
+    g.remote_dma_fused(
+        [RemoteDMATransfer(dst_ids=[dst(d)], dma_engine_mask=_mask(in_e[k_near * i:k_near * (i + 1)]),
+                           remote_sem=sem.near, src=T.gath[:, W * d:W * d + W],
+                           dst=T.land[:, W * rank:W * rank + W]) for i, d in enumerate(peers)],
+        local_sem=sem.sent)
+    sent += k_near * len(peers)
+    for q in clients:
+        g.wait_ge(sem.rel, k_stage)
+        g.remote_dma_fused(
+            [RemoteDMATransfer(dst_ids=[dst(d)], dma_engine_mask=_mask(out_e[k_far * i:k_far * (i + 1)]),
+                               remote_sem=sem.farr, src=T.stage[:, W * i:W * i + W],
+                               dst=T.land[:, W * q:W * q + W]) for i, d in enumerate(far)],
+            local_sem=sem.sent)
+        sent += k_far * len(far)
+
+    came = [q for q in far if direct(q)]
+    passed = [q for q in far if not direct(q)]
+    g.scalar.wait_ge(sem.s_own, 1)
+    g.scalar.wait_ge(sem.near, k_near * len(peers))
+    g.scalar.dma_start(T.y[:, W * h0:W * h1], T.land[:, W * h0:W * h1]).then_inc(sem.st_a, 16)
+    g.scalar.wait_ge(sem.fard, k_far * len(came))
+    nb = 0
+    for a, b in _runs(came):
+        g.scalar.dma_start(T.y[:, W * a:W * b], T.land[:, W * a:W * b]).then_inc(sem.st_b, 16)
+        nb += 16
+    g.sync.wait_ge(sem.farr, k_far * len(passed))
+    nc = 0
+    for a, b in _runs(passed):
+        g.sync.dma_start(T.y[:, W * a:W * b], T.land[:, W * a:W * b]).then_inc(sem.st_c, 16)
+        nc += 16
+    g.scalar.wait_ge(sem.st_a, 16)
+    g.scalar.wait_ge(sem.st_b, nb)
+    g.sync.wait_ge(sem.st_c, nc)
+    g.wait_ge(sem.sent, sent)

@@ -1,23 +1,22 @@
 from concourse.bass import DstId, RemoteDMATransfer
-from concourse.mybir import AluOpType
 
 W = 32
 GRP = 16
+HALVES = 2
 
 SCRATCH = {
-    "xs":    ("sbuf", [128, 256], "float32"),
-    "l32":   ("sbuf", [128, 16], "int32"),
-    "lf":    ("sbuf", [128, 16], "float32"),
-    "ones":  ("sbuf", [128, 128], "float32"),
-    "rep":   ("sbuf", [128, 128], "float32"),
-    "offp":  ("psum", [128, 16], "float32"),
-    "off":   ("sbuf", [128, 16], "uint16"),
-    "gath":  ("sbuf", [128, 256], "float32"),
-    "stage": ("sbuf", [128, 128], "float32"),
-    "land":  ("sbuf", [128, 256], "float32"),
+    "xs":     ("sbuf", [128, 256], "float32"),
+    "l32":    ("sbuf", [128, 16], "int32"),
+    "off":    ("sbuf", [128, 16], "uint16"),
+    "gath":   ("sbuf", [128, 256], "float32"),
+    "stage":  ("sbuf", [128, 64], "float32"),
+    "dstage": ("dram", [2, 128, 32], "float32"),
+    "land":   ("sbuf", [128, 256], "float32"),
+    "dland":  ("dram", [2, 128, 32], "float32"),
 }
-SEMAPHORES = ["s_x", "s_l", "s_one", "s_rep", "s_lf", "s_mm", "s_off", "s_gf", "s_gn", "s_own",
-              "near", "fard", "farr", "rel", "sent", "st_a", "st_b", "st_c"]
+SEMAPHORES = ["s_x", "s_l", "s_off", "s_gf0", "s_gf1", "s_gn", "s_own",
+              "near", "fard", "farr", "farr0", "farr1", "rel0", "rel1", "sent", "st_a", "st_b", "st_c", "st_c0",
+              "st_c1"]
 
 
 def _bits(mask):
@@ -65,12 +64,17 @@ def rank_program(g, core, T, topo):
         rest = [q for q in chipmates(r) if not direct(q)]
         return ports[rest.index(r) % len(ports)]
 
+    def passed_of(r):
+        return [q for q in others(r) if not direct(q)]
+
     home = chipmates(rank)
     far = others(rank)
     (f0, f1), = _runs(far)
     (h0, h1), = _runs(home)
     clients = [q for q in home if q != rank and gate(q) == rank]
     assert len(clients) <= 1
+    per = len(far) // HALVES
+    first, second = far[:per], far[per:]
 
     def dst(r):
         rid, pid, _ = topo.addr(cores[r])
@@ -80,46 +84,55 @@ def rank_program(g, core, T, topo):
     all_e = _bits(topo.mask(core, cores[peers[0]]))
     out_e = _bits(topo.mask(core, cores[far[0]]))
     in_e = [e for e in all_e if e not in out_e]
-    k_far = len(out_e) // len(far)
+    k_fwd = len(out_e) // per
     k_near = 2
-    k_stage = len(out_e)
+    stage_e = all_e[:len(out_e)]
+    k_stage = len(stage_e)
+    k_slot = k_stage // per
 
     g.sync.dma_start(T.xs[:, :], T.x[:, :]).then_inc(sem.s_x, 16)
-    g.scalar.dma_start(T.l32[0:GRP, :], T.l[:, :]).then_inc(sem.s_l, 16)
-
-    g.vector.memset(T.ones[0:GRP, :], 1.0).then_inc(sem.s_one, 1)
-    g.wait_ge(sem.s_one, 1)
-    g.affine_select(T.rep[0:GRP, :], T.ones[0:GRP, :], [[0, 128 // GRP], [-1, GRP]], AluOpType.is_equal, 0.0, 0,
-                    1).then_inc(sem.s_rep, 1)
-    g.vector.wait_ge(sem.s_l, 16)
-    g.vector.tensor_copy(T.lf[0:GRP, :], T.l32[0:GRP, :]).then_inc(sem.s_lf, 1)
-    g.tensor.wait_ge(sem.s_rep, 1)
-    g.tensor.wait_ge(sem.s_lf, 1)
-    g.tensor.matmul(T.offp[:, :], T.rep[0:GRP, :], T.lf[0:GRP, :], True, True).then_inc(sem.s_mm, 1)
-    g.vector.wait_ge(sem.s_mm, 1)
-    g.vector.tensor_copy(T.off[:, :], T.offp[:, :]).then_inc(sem.s_off, 1)
+    groups = 128 // GRP
+    for k in range(groups):
+        queue = g.scalar if k < 5 else g.sync
+        queue.dma_start(T.l32[GRP * k:GRP * (k + 1), :], T.l[:, :]).then_inc(sem.s_l, 16)
+    g.vector.wait_ge(sem.s_l, 16 * groups)
+    g.vector.tensor_copy(T.off[:, :], T.l32[:, :]).then_inc(sem.s_off, 1)
 
     c = W // GRP
+
+    def gather(out, a, b):
+        return g.vector.tensor_copy(out, T.xs[:, :].indirect(T.off[:, c * a:c * b]))
+
     g.vector.wait_ge(sem.s_off, 1)
     g.vector.wait_ge(sem.s_x, 16)
-    g.vector.tensor_copy(T.gath[:, W * f0:W * f1], T.xs[:, :].indirect(T.off[:, c * f0:c * f1])).then_inc(sem.s_gf, 1)
-    g.vector.tensor_copy(T.gath[:, W * h0:W * h1], T.xs[:, :].indirect(T.off[:, c * h0:c * h1])).then_inc(sem.s_gn, 1)
-    g.vector.tensor_copy(T.land[:, W * rank:W * rank + W],
-                         T.xs[:, :].indirect(T.off[:, c * rank:c * rank + c])).then_inc(sem.s_own, 1)
+    for j, piece in enumerate([first, second]):
+        a, b = piece[0], piece[-1] + 1
+        gather(T.gath[:, W * a:W * b], a, b).then_inc(sem["s_gf%d" % j], 1)
+    gather(T.gath[:, W * h0:W * h1], h0, h1).then_inc(sem.s_gn, 1)
+    gather(T.land[:, W * rank:W * rank + W], rank, rank + 1).then_inc(sem.s_own, 1)
 
     sent = 0
-    g.wait_ge(sem.s_gf, 1)
     if direct(rank):
-        g.remote_dma_fused(
-            [RemoteDMATransfer(dst_ids=[dst(d)], dma_engine_mask=_mask(out_e[k_far * i:k_far * (i + 1)]),
-                               remote_sem=sem.fard, src=T.gath[:, W * d:W * d + W],
-                               dst=T.land[:, W * rank:W * rank + W]) for i, d in enumerate(far)],
-            local_sem=sem.sent)
-        sent += k_far * len(far)
+        for j, piece in enumerate([first, second]):
+            g.wait_ge(sem["s_gf%d" % j], 1)
+            g.remote_dma_fused(
+                [RemoteDMATransfer(dst_ids=[dst(d)], dma_engine_mask=_mask(out_e[k_fwd * i:k_fwd * (i + 1)]),
+                                   remote_sem=sem.fard, src=T.gath[:, W * d:W * d + W],
+                                   dst=T.land[:, W * rank:W * rank + W]) for i, d in enumerate(piece)],
+                local_sem=sem.sent)
+            sent += k_fwd * per
     else:
         rid, pid, _ = topo.addr(cores[gate(rank)])
-        g.remote_dma(T.stage[:, :], T.gath[:, W * f0:W * f1], sem.rel, sem.sent, pid, rid, _mask(all_e[:k_stage]))
-        sent += k_stage
+        g.wait_ge(sem.s_gf0, 1)
+        g.remote_dma(T.stage[:, :], T.gath[:, W * first[0]:W * (first[-1] + 1)], sem.rel0, sem.sent, pid, rid,
+                     _mask(stage_e))
+        g.wait_ge(sem.s_gf1, 1)
+        g.remote_dma_fused(
+            [RemoteDMATransfer(dst_ids=[dst(gate(rank))], dma_engine_mask=_mask(stage_e[k_slot * i:k_slot * (i + 1)]),
+                               remote_sem=sem.rel1, src=T.gath[:, W * d:W * d + W], dst=T.dstage[i])
+             for i, d in enumerate(second)],
+            local_sem=sem.sent)
+        sent += 2 * k_stage
     g.wait_ge(sem.s_gn, 1)
     g.remote_dma_fused(
         [RemoteDMATransfer(dst_ids=[dst(d)], dma_engine_mask=_mask(in_e[k_near * i:k_near * (i + 1)]),
@@ -128,30 +141,45 @@ def rank_program(g, core, T, topo):
         local_sem=sem.sent)
     sent += k_near * len(peers)
     for q in clients:
-        g.wait_ge(sem.rel, k_stage)
+        g.wait_ge(sem.rel0, k_stage)
         g.remote_dma_fused(
-            [RemoteDMATransfer(dst_ids=[dst(d)], dma_engine_mask=_mask(out_e[k_far * i:k_far * (i + 1)]),
+            [RemoteDMATransfer(dst_ids=[dst(d)], dma_engine_mask=_mask(out_e[k_fwd * i:k_fwd * (i + 1)]),
                                remote_sem=sem.farr, src=T.stage[:, W * i:W * i + W],
-                               dst=T.land[:, W * q:W * q + W]) for i, d in enumerate(far)],
+                               dst=T.land[:, W * q:W * q + W]) for i, d in enumerate(first)],
             local_sem=sem.sent)
-        sent += k_far * len(far)
+        g.wait_ge(sem.rel1, k_stage)
+        g.remote_dma_fused(
+            [RemoteDMATransfer(dst_ids=[dst(d)], dma_engine_mask=_mask(out_e[k_fwd * i:k_fwd * (i + 1)]),
+                               remote_sem=sem["farr%d" % passed_of(d).index(q)], src=T.dstage[i],
+                               dst=T.dland[passed_of(d).index(q)]) for i, d in enumerate(second)],
+            local_sem=sem.sent)
+        sent += 2 * k_fwd * per
 
     came = [q for q in far if direct(q)]
-    passed = [q for q in far if not direct(q)]
+    passed = passed_of(rank)
     g.scalar.wait_ge(sem.s_own, 1)
     g.scalar.wait_ge(sem.near, k_near * len(peers))
     g.scalar.dma_start(T.y[:, W * h0:W * h1], T.land[:, W * h0:W * h1]).then_inc(sem.st_a, 16)
-    g.scalar.wait_ge(sem.fard, k_far * len(came))
+    g.scalar.wait_ge(sem.fard, k_fwd * len(came))
     nb = 0
     for a, b in _runs(came):
         g.scalar.dma_start(T.y[:, W * a:W * b], T.land[:, W * a:W * b]).then_inc(sem.st_b, 16)
         nb += 16
-    g.sync.wait_ge(sem.farr, k_far * len(passed))
-    nc = 0
-    for a, b in _runs(passed):
-        g.sync.dma_start(T.y[:, W * a:W * b], T.land[:, W * a:W * b]).then_inc(sem.st_c, 16)
-        nc += 16
+    if home.index(rank) < per:
+        g.sync.wait_ge(sem.farr, k_fwd * len(passed))
+        nc = 0
+        for a, b in _runs(passed):
+            g.sync.dma_start(T.y[:, W * a:W * b], T.land[:, W * a:W * b]).then_inc(sem.st_c, 16)
+            nc += 16
+        g.sync.wait_ge(sem.st_c, nc)
+    else:
+        assert len(passed) == 2
+        for k, queue in enumerate((g.sync, g.scalar)):
+            q = passed[k]
+            queue.wait_ge(sem["farr%d" % k], k_fwd)
+            queue.dma_start(T.y[:, W * q:W * q + W], T.dland[k]).then_inc(sem["st_c%d" % k], 16)
+        g.sync.wait_ge(sem.st_c0, 16)
+        g.scalar.wait_ge(sem.st_c1, 16)
     g.scalar.wait_ge(sem.st_a, 16)
     g.scalar.wait_ge(sem.st_b, nb)
-    g.sync.wait_ge(sem.st_c, nc)
     g.wait_ge(sem.sent, sent)

@@ -7,6 +7,9 @@ HALVES = 2
 SCRATCH = {
     "xs":     ("sbuf", [128, 256], "float32"),
     "l32":    ("sbuf", [128, 16], "int32"),
+    "cl32":   ("sbuf", [128, 2], "int32"),
+    "coff":   ("sbuf", [128, 2], "uint16"),
+    "cx":     ("sbuf", [128, 256], "float32"),
     "off":    ("sbuf", [128, 16], "uint16"),
     "gath":   ("sbuf", [128, 256], "float32"),
     "stage":  ("sbuf", [128, 64], "float32"),
@@ -14,7 +17,7 @@ SCRATCH = {
     "land":   ("sbuf", [128, 256], "float32"),
     "dland":  ("dram", [2, 128, 32], "float32"),
 }
-SEMAPHORES = ["s_x", "s_l", "s_off", "s_gf0", "s_gf1", "s_gn", "s_own",
+SEMAPHORES = ["s_x", "s_l", "s_off", "s_gf0", "s_gf1", "s_gn", "s_own", "s_coff", "s_pg", "rl", "relx",
               "near", "fard", "farr", "farr0", "farr1", "rel0", "rel1", "sent", "st_a", "st_b", "st_c", "st_c0",
               "st_c1"]
 
@@ -61,8 +64,8 @@ def rank_program(g, core, T, topo):
         if direct(r):
             return r
         ports = [q for q in chipmates(r) if direct(q)]
-        rest = [q for q in chipmates(r) if not direct(q)]
-        return ports[rest.index(r) % len(ports)]
+        rest_ = [q for q in chipmates(r) if not direct(q)]
+        return ports[rest_.index(r) % len(ports)]
 
     def passed_of(r):
         return [q for q in others(r) if not direct(q)]
@@ -85,16 +88,18 @@ def rank_program(g, core, T, topo):
     out_e = _bits(topo.mask(core, cores[far[0]]))
     in_e = [e for e in all_e if e not in out_e]
     k_fwd = len(out_e) // per
-    k_near = 2
+    k_near = 4
+    partner = clients[0] if direct(rank) else gate(rank)
+    rest = [q for q in peers if q != partner]
     stage_e = all_e[:len(out_e)]
     k_stage = len(stage_e)
     k_slot = k_stage // per
 
-    g.sync.dma_start(T.xs[:, :], T.x[:, :]).then_inc(sem.s_x, 16)
     groups = 128 // GRP
     for k in range(groups):
-        queue = g.scalar if k < 5 else g.sync
+        queue = g.scalar if k % 2 else g.sync
         queue.dma_start(T.l32[GRP * k:GRP * (k + 1), :], T.l[:, :]).then_inc(sem.s_l, 16)
+    g.sync.dma_start(T.xs[:, :], T.x[:, :]).then_inc(sem.s_x, 16)
     g.vector.wait_ge(sem.s_l, 16 * groups)
     g.vector.tensor_copy(T.off[:, :], T.l32[:, :]).then_inc(sem.s_off, 1)
 
@@ -110,9 +115,26 @@ def rank_program(g, core, T, topo):
         gather(T.gath[:, W * a:W * b], a, b).then_inc(sem["s_gf%d" % j], 1)
     gather(T.gath[:, W * h0:W * h1], h0, h1).then_inc(sem.s_gn, 1)
     gather(T.land[:, W * rank:W * rank + W], rank, rank + 1).then_inc(sem.s_own, 1)
+    g.vector.wait_ge(sem.rl, k_stage)
+    g.vector.tensor_copy(T.coff[:, :], T.cl32[:, :]).then_inc(sem.s_coff, 1)
+    g.vector.wait_ge(sem.s_coff, 1)
+    g.vector.wait_ge(sem.relx, len(in_e))
+    g.vector.tensor_copy(T.land[:, W * partner:W * partner + W],
+                         T.cx[:, :].indirect(T.coff[:, :])).then_inc(sem.s_pg, 1)
 
     sent = 0
+    prid, ppid, _ = topo.addr(cores[partner])
+    g.wait_ge(sem.s_l, 16 * groups)
+    g.remote_dma(T.cl32[:, :], T.l32[:, c * partner:c * partner + c], sem.rl, sem.sent, ppid, prid, _mask(stage_e))
+    sent += k_stage
+
+    def send_x():
+        g.wait_ge(sem.s_x, 16)
+        g.remote_dma(T.cx[:, :], T.xs[:, :], sem.relx, sem.sent, ppid, prid, _mask(in_e))
+
+    sent += len(in_e)
     if direct(rank):
+        send_x()
         for j, piece in enumerate([first, second]):
             g.wait_ge(sem["s_gf%d" % j], 1)
             g.remote_dma_fused(
@@ -133,13 +155,16 @@ def rank_program(g, core, T, topo):
              for i, d in enumerate(second)],
             local_sem=sem.sent)
         sent += 2 * k_stage
+        send_x()
+
+    near_e = in_e if direct(rank) else stage_e
     g.wait_ge(sem.s_gn, 1)
     g.remote_dma_fused(
-        [RemoteDMATransfer(dst_ids=[dst(d)], dma_engine_mask=_mask(in_e[k_near * i:k_near * (i + 1)]),
+        [RemoteDMATransfer(dst_ids=[dst(d)], dma_engine_mask=_mask(near_e[k_near * i:k_near * (i + 1)]),
                            remote_sem=sem.near, src=T.gath[:, W * d:W * d + W],
-                           dst=T.land[:, W * rank:W * rank + W]) for i, d in enumerate(peers)],
+                           dst=T.land[:, W * rank:W * rank + W]) for i, d in enumerate(rest)],
         local_sem=sem.sent)
-    sent += k_near * len(peers)
+    sent += k_near * len(rest)
     for q in clients:
         g.wait_ge(sem.rel0, k_stage)
         g.remote_dma_fused(
@@ -157,14 +182,15 @@ def rank_program(g, core, T, topo):
 
     came = [q for q in far if direct(q)]
     passed = passed_of(rank)
-    g.scalar.wait_ge(sem.s_own, 1)
-    g.scalar.wait_ge(sem.near, k_near * len(peers))
-    g.scalar.dma_start(T.y[:, W * h0:W * h1], T.land[:, W * h0:W * h1]).then_inc(sem.st_a, 16)
     g.scalar.wait_ge(sem.fard, k_fwd * len(came))
     nb = 0
     for a, b in _runs(came):
         g.scalar.dma_start(T.y[:, W * a:W * b], T.land[:, W * a:W * b]).then_inc(sem.st_b, 16)
         nb += 16
+    g.scalar.wait_ge(sem.s_own, 1)
+    g.scalar.wait_ge(sem.s_pg, 1)
+    g.scalar.wait_ge(sem.near, k_near * len(rest))
+    g.scalar.dma_start(T.y[:, W * h0:W * h1], T.land[:, W * h0:W * h1]).then_inc(sem.st_a, 16)
     if home.index(rank) < per:
         g.sync.wait_ge(sem.farr, k_fwd * len(passed))
         nc = 0

from concourse.bass import DstId, RemoteDMATransfer

W = 32
GRP = 16
HALVES = 2

SCRATCH = {
    "xs":     ("sbuf", [128, 256], "float32"),
    "l32":    ("sbuf", [128, 16], "int32"),
    "cl32":   ("sbuf", [128, 2], "int32"),
    "coff":   ("sbuf", [128, 2], "uint16"),
    "cx":     ("sbuf", [128, 256], "float32"),
    "off":    ("sbuf", [128, 16], "uint16"),
    "gath":   ("sbuf", [128, 256], "float32"),
    "stage":  ("sbuf", [128, 64], "float32"),
    "dstage": ("dram", [2, 128, 32], "float32"),
    "land":   ("sbuf", [128, 256], "float32"),
    "dland":  ("dram", [2, 128, 32], "float32"),
}
SEMAPHORES = ["s_x", "s_l", "s_off", "s_gf0", "s_gf1", "s_gn", "s_own", "s_coff", "s_pg", "rl", "relx",
              "near", "fard", "farr", "farr0", "farr1", "rel0", "rel1", "sent", "st_a", "st_b", "st_c", "st_c0",
              "st_c1"]


def _bits(mask):
    return [e for e in range(mask.bit_length()) if (mask >> e) & 1]


def _mask(engines):
    m = 0
    for e in engines:
        m |= 1 << e
    return m


def _runs(ranks):
    out = []
    for r in sorted(ranks):
        if out and out[-1][1] == r:
            out[-1][1] = r + 1
        else:
            out.append([r, r + 1])
    return [(a, b) for a, b in out]


def rank_program(g, core, T, topo):
    rank = T.rank_of(core)
    if rank is None:
        return
    cores = list(T.cores)
    n = len(cores)
    sem = T.sem

    def chipmates(r):
        return [q for q in range(n) if topo.chip(cores[q]) == topo.chip(cores[r])]

    def others(r):
        return [q for q in range(n) if topo.chip(cores[q]) != topo.chip(cores[r])]

    def direct(r):
        return all(topo.may_write(cores[r], cores[q]) for q in others(r))

    def gate(r):
        if direct(r):
            return r
        ports = [q for q in chipmates(r) if direct(q)]
        rest_ = [q for q in chipmates(r) if not direct(q)]
        return ports[rest_.index(r) % len(ports)]

    def passed_of(r):
        return [q for q in others(r) if not direct(q)]

    home = chipmates(rank)
    far = others(rank)
    (f0, f1), = _runs(far)
    (h0, h1), = _runs(home)
    clients = [q for q in home if q != rank and gate(q) == rank]
    assert len(clients) <= 1
    per = len(far) // HALVES
    first, second = far[:per], far[per:]

    def dst(r):
        rid, pid, _ = topo.addr(cores[r])
        return DstId(rid=rid, pnc=pid)

    peers = [q for q in home if q != rank]
    all_e = _bits(topo.mask(core, cores[peers[0]]))
    out_e = _bits(topo.mask(core, cores[far[0]]))
    in_e = [e for e in all_e if e not in out_e]
    k_fwd = len(out_e) // per
    k_near = 4
    partner = clients[0] if direct(rank) else gate(rank)
    rest = [q for q in peers if q != partner]
    stage_e = all_e[:len(out_e)]
    k_stage = len(stage_e)
    k_slot = k_stage // per

    groups = 128 // GRP
    for k in range(groups):
        queue = g.scalar if k % 2 else g.sync
        queue.dma_start(T.l32[GRP * k:GRP * (k + 1), :], T.l[:, :]).then_inc(sem.s_l, 16)
    g.sync.dma_start(T.xs[:, :], T.x[:, :]).then_inc(sem.s_x, 16)
    g.vector.wait_ge(sem.s_l, 16 * groups)
    g.vector.tensor_copy(T.off[:, :], T.l32[:, :]).then_inc(sem.s_off, 1)

    c = W // GRP

    def gather(out, a, b):
        return g.vector.tensor_copy(out, T.xs[:, :].indirect(T.off[:, c * a:c * b]))

    g.vector.wait_ge(sem.s_off, 1)
    g.vector.wait_ge(sem.s_x, 16)
    for j, piece in enumerate([first, second]):
        a, b = piece[0], piece[-1] + 1
        gather(T.gath[:, W * a:W * b], a, b).then_inc(sem["s_gf%d" % j], 1)
    gather(T.gath[:, W * h0:W * h1], h0, h1).then_inc(sem.s_gn, 1)
    gather(T.land[:, W * rank:W * rank + W], rank, rank + 1).then_inc(sem.s_own, 1)
    g.vector.wait_ge(sem.rl, k_stage)
    g.vector.tensor_copy(T.coff[:, :], T.cl32[:, :]).then_inc(sem.s_coff, 1)
    g.vector.wait_ge(sem.s_coff, 1)
    g.vector.wait_ge(sem.relx, len(in_e))
    g.vector.tensor_copy(T.land[:, W * partner:W * partner + W],
                         T.cx[:, :].indirect(T.coff[:, :])).then_inc(sem.s_pg, 1)

    sent = 0
    prid, ppid, _ = topo.addr(cores[partner])
    g.wait_ge(sem.s_l, 16 * groups)
    g.remote_dma(T.cl32[:, :], T.l32[:, c * partner:c * partner + c], sem.rl, sem.sent, ppid, prid, _mask(stage_e))
    sent += k_stage

    def send_x():
        g.wait_ge(sem.s_x, 16)
        g.remote_dma(T.cx[:, :], T.xs[:, :], sem.relx, sem.sent, ppid, prid, _mask(in_e))

    sent += len(in_e)
    if direct(rank):
        send_x()
        for j, piece in enumerate([first, second]):
            g.wait_ge(sem["s_gf%d" % j], 1)
            g.remote_dma_fused(
                [RemoteDMATransfer(dst_ids=[dst(d)], dma_engine_mask=_mask(out_e[k_fwd * i:k_fwd * (i + 1)]),
                                   remote_sem=sem.fard, src=T.gath[:, W * d:W * d + W],
                                   dst=T.land[:, W * rank:W * rank + W]) for i, d in enumerate(piece)],
                local_sem=sem.sent)
            sent += k_fwd * per
    else:
        rid, pid, _ = topo.addr(cores[gate(rank)])
        g.wait_ge(sem.s_gf0, 1)
        g.remote_dma(T.stage[:, :], T.gath[:, W * first[0]:W * (first[-1] + 1)], sem.rel0, sem.sent, pid, rid,
                     _mask(stage_e))
        g.wait_ge(sem.s_gf1, 1)
        g.remote_dma_fused(
            [RemoteDMATransfer(dst_ids=[dst(gate(rank))], dma_engine_mask=_mask(stage_e[k_slot * i:k_slot * (i + 1)]),
                               remote_sem=sem.rel1, src=T.gath[:, W * d:W * d + W], dst=T.dstage[i])
             for i, d in enumerate(second)],
            local_sem=sem.sent)
        sent += 2 * k_stage
        send_x()

    near_e = in_e if direct(rank) else stage_e
    g.wait_ge(sem.s_gn, 1)
    g.remote_dma_fused(
        [RemoteDMATransfer(dst_ids=[dst(d)], dma_engine_mask=_mask(near_e[k_near * i:k_near * (i + 1)]),
                           remote_sem=sem.near, src=T.gath[:, W * d:W * d + W],
                           dst=T.land[:, W * rank:W * rank + W]) for i, d in enumerate(rest)],
        local_sem=sem.sent)
    sent += k_near * len(rest)
    for q in clients:
        g.wait_ge(sem.rel0, k_stage)
        g.remote_dma_fused(
            [RemoteDMATransfer(dst_ids=[dst(d)], dma_engine_mask=_mask(out_e[k_fwd * i:k_fwd * (i + 1)]),
                               remote_sem=sem.farr, src=T.stage[:, W * i:W * i + W],
                               dst=T.land[:, W * q:W * q + W]) for i, d in enumerate(first)],
            local_sem=sem.sent)
        g.wait_ge(sem.rel1, k_stage)
        g.remote_dma_fused(
            [RemoteDMATransfer(dst_ids=[dst(d)], dma_engine_mask=_mask(out_e[k_fwd * i:k_fwd * (i + 1)]),
                               remote_sem=sem["farr%d" % passed_of(d).index(q)], src=T.dstage[i],
                               dst=T.dland[passed_of(d).index(q)]) for i, d in enumerate(second)],
            local_sem=sem.sent)
        sent += 2 * k_fwd * per

    came = [q for q in far if direct(q)]
    passed = passed_of(rank)
    g.scalar.wait_ge(sem.fard, k_fwd * len(came))
    nb = 0
    for a, b in _runs(came):
        g.scalar.dma_start(T.y[:, W * a:W * b], T.land[:, W * a:W * b]).then_inc(sem.st_b, 16)
        nb += 16
    g.scalar.wait_ge(sem.s_own, 1)
    g.scalar.wait_ge(sem.s_pg, 1)
    g.scalar.wait_ge(sem.near, k_near * len(rest))
    g.scalar.dma_start(T.y[:, W * h0:W * h1], T.land[:, W * h0:W * h1]).then_inc(sem.st_a, 16)
    if home.index(rank) < per:
        g.sync.wait_ge(sem.farr, k_fwd * len(passed))
        nc = 0
        for a, b in _runs(passed):
            g.sync.dma_start(T.y[:, W * a:W * b], T.land[:, W * a:W * b]).then_inc(sem.st_c, 16)
            nc += 16
        g.sync.wait_ge(sem.st_c, nc)
    else:
        assert len(passed) == 2
        for k, queue in enumerate((g.sync, g.scalar)):
            q = passed[k]
            queue.wait_ge(sem["farr%d" % k], k_fwd)
            queue.dma_start(T.y[:, W * q:W * q + W], T.dland[k]).then_inc(sem["st_c%d" % k], 16)
        g.sync.wait_ge(sem.st_c0, 16)
        g.scalar.wait_ge(sem.st_c1, 16)
    g.scalar.wait_ge(sem.st_a, 16)
    g.scalar.wait_ge(sem.st_b, nb)
    g.wait_ge(sem.sent, sent)
